import numpy as np
import ml_dtypes


def mxq(x, axis, fmt="e4m3"):
    dtype, down = {"e4m3": (ml_dtypes.float8_e4m3fn, 7), "e5m2": (ml_dtypes.float8_e5m2, 14)}[fmt]
    v = np.moveaxis(np.asarray(x, np.float32).astype(ml_dtypes.bfloat16).astype(np.float64), axis, -1)
    blocks = v.reshape(v.shape[:-1] + (-1, 32))
    amax = np.abs(blocks).max(-1, keepdims=True)
    byte = np.maximum(np.where(amax > 0, np.frexp(amax)[1] - 1 + 127, 0) - down, 1)
    scale = np.exp2(byte - 127.0)
    codes = (blocks / scale).astype(np.float32).astype(dtype).astype(np.float64)
    return np.moveaxis((codes * scale).reshape(v.shape), -1, axis)


WIDE = False


def mx_kscale(k):
    if not WIDE:
        return np.ones(k)
    levels = np.array([10, -10, 5, -5, 0])
    if k % 512:
        return np.exp2(np.random.permutation(np.resize(levels, k // 32))).repeat(32)
    a = np.empty((k // 512, 16))
    for p in range(k // 512):
        a[p, :8] = np.random.permutation(np.resize(levels, 8))
        for g in range(8):
            far = levels[np.abs(levels - a[p, g]) >= 10]
            a[p, g + 8] = far[np.random.randint(len(far))]
    return np.exp2(a.ravel()).repeat(32)


def f64(x):
    return np.asarray(x).astype(np.float64)


def striped(idx):
    return np.tile(idx.reshape(-1, 16).T, (8, 1)).astype(np.uint16)


def unstriped(offs):
    return offs[:16].T.reshape(-1).astype(np.int64)


E2M1 = np.array([0.0, 0.5, 1.0, 1.5, 2.0, 3.0, 4.0, 6.0, -0.0, -0.5, -1.0, -1.5, -2.0, -3.0, -4.0, -6.0])


def pack_weight(w, fmt):
    k, n = w.shape
    w = f64(np.asarray(w, np.float32).astype(ml_dtypes.bfloat16)).reshape(k // 32, 32, n)
    amax = np.abs(w).max(1)
    if fmt == "e4m3":
        byte = np.frexp(amax)[1] - 1 + 127 - 7
    else:
        mant, ex = np.frexp(amax / 6.0)
        byte = np.where(mant > 0.5, ex, ex - 1) + 127
    byte = np.clip(np.where(amax > 0, byte, 1), 1, 254)
    scaled = (w * np.exp2(127.0 - byte)[:, None, :]).reshape(k, n).astype(np.float32)
    by_word = np.ascontiguousarray(scaled.reshape(k // 512, 128, 4, n).transpose(0, 1, 3, 2))
    if fmt == "e4m3":
        words = by_word.astype(ml_dtypes.float8_e4m3fn).view(np.uint8)
    else:
        c = by_word.astype(ml_dtypes.float4_e2m1fn).view(np.uint8) & 0xF
        words = (c[..., 0::2] | (c[..., 1::2] << 4)).reshape(k // 512, 128, 2 * n)
    return np.ascontiguousarray(words), np.ascontiguousarray(byte.astype(np.uint8).reshape(k // 512, 16, n))


def unpack_weight(words, scales, fmt):
    g, _, n = scales.shape
    words = np.ascontiguousarray(words).reshape(g, 128, n, -1)
    if fmt == "e4m3":
        vals = words.view(ml_dtypes.float8_e4m3fn).astype(np.float64)
    else:
        nib = np.empty((g, 128, n, 4), np.uint8)
        nib[..., 0::2] = words & 0xF
        nib[..., 1::2] = words >> 4
        vals = E2M1[nib]
    vals = vals * np.repeat(np.exp2(scales.astype(np.float64) - 127.0), 8, axis=1)[..., None]
    return vals.transpose(0, 1, 3, 2).reshape(g * 512, n)


def gelu(v):
    return 0.5 * v * (1.0 + np.tanh(np.sqrt(2.0 / np.pi) * (v + 0.044715 * v**3)))


def striped8(idx):
    return np.concatenate([v.reshape(-1, 16).T for v in idx]).astype(np.uint16)


def unstriped8(offs):
    return np.stack([offs[16 * g:16 * g + 16].T.reshape(-1) for g in range(8)]).astype(np.int64)


def runs(v, idx8):
    k = np.arange(v.shape[0])
    return v[k[:, None], idx8[k % 512 // 64]]


def often(T, S):
    return np.random.permutation(T)[(T * np.random.uniform(0, 1, S) ** 4).astype(np.int64)]


K, H, N, T, S, P = 1024, 1024, 512, 2048, 1024, 512


def setup_inputs():
    n = np.random.standard_normal
    s = mx_kscale(K)[:, None]
    u = mx_kscale(H)[:, None]
    d = {}
    d["tab_words"], d["tab_scales"] = pack_weight(n((K, T)) * s, "e4m3")
    d["offs"] = striped8(np.stack([often(T, S) for _ in range(8)]))
    d["pos1"] = striped(np.random.permutation(S)[:P])
    d["pos2"] = striped(np.random.permutation(S)[:P])
    d["w1"] = (n((K, H)) / s / K ** 0.5).astype(np.float32)
    base = np.exp(0.3 * n(H)) * u[:, 0]
    d["gain"] = base.astype(np.float32)
    d["rate"] = (np.random.uniform(0.42, 0.55, H) / base).astype(np.float32)
    d["w2"] = (n((H, N)) / u / H ** 0.5).astype(np.float32)
    d["w3_words"], d["w3_scales"] = pack_weight(n((H, N)) / u / H ** 0.5, "e2m1")
    d["load"] = np.exp(0.5 * n((N, P))).astype(np.float32)
    return d


def reference(tab_words, tab_scales, offs, pos1, pos2, w1, gain, rate, w2, w3_words, w3_scales, load):
    v = runs(unpack_weight(tab_words, tab_scales, "e4m3"), unstriped8(offs))
    h = f64(gain)[:, None] * (mxq(f64(w1), 0, "e4m3").T @ v)
    x1 = h[:, unstriped(pos1)]
    x2 = h[:, unstriped(pos2)]
    z = np.cos(f64(rate)[:, None] * x1) * x2
    turned = mxq(f64(w2), 0, "e4m3").T @ mxq(z, 0, "e4m3")
    direct = unpack_weight(w3_words, w3_scales, "e2m1").T @ mxq(x2, 0, "e4m3")
    return f64(load) * turned + direct

@@ -1,0 +1,250 @@
+import math
+from contextlib import ExitStack
+
+import concourse.mybir as mybir
+
+K, H, N, T, S, J = 1024, 1024, 512, 2048, 1024, 512
+FLOPS = 2 * K * H * S + 2 * 2 * H * N * J
+
+F32 = mybir.dt.float32
+BF16 = mybir.dt.bfloat16
+I32 = mybir.dt.int32
+U32 = mybir.dt.uint32
+U16 = mybir.dt.uint16
+U8 = mybir.dt.uint8
+FP8X4 = mybir.dt.float8_e4m3fn_x4
+FP4X4 = mybir.dt.float4_e2m1fn_x4
+ACT = mybir.ActivationFunctionType
+ALU = mybir.AluOpType
+
+P = 128
+PACK = 4
+PASS = P * PACK
+BANK = 512
+PLANE_STEP = 8
+W1_VECTOR_SHARE = (32, 64)
+
+
+def tile_list_aligner_stage_forces_kernel(
+    tc, tab_words, tab_scales, offs, pos1, pos2, w1, gain, rate, w2, w3_words, w3_scales, load, out
+):
+    nc = tc.nc
+    with ExitStack() as ctx:
+        keep = ctx.enter_context(tc.tile_pool(name="keep", bufs=1))
+        stage = ctx.enter_context(tc.tile_pool(name="stage", bufs=4))
+        psum = ctx.enter_context(tc.psum_pool(name="psum", bufs=1))
+
+        def bank(i, name):
+            return psum.tile([P, BANK], F32, name=name, tag="bank%d" % i)
+
+        def staged(shape, dtype, name):
+            return stage.tile(shape, dtype, name=name, tag="stage", align_bytes=64)
+
+        def mx_tiles(name, width):
+            codes = keep.tile([P, width], U32, name=name + "_codes", align_bytes=64)
+            scales = keep.tile([P, width], U8, name=name + "_scales", align_bytes=64)
+            return codes, scales
+
+        def quantize(grouped, name):
+            codes, scales = mx_tiles(name, BANK)
+            nc.vector.quantize_mx(out=codes[:].bitcast(FP8X4), scales=scales[:], in_=grouped)
+            return codes, scales
+
+        offs_sb = keep.tile([P, S // 16], U16, name="offs_sb")
+        nc.sync.dma_start(offs_sb[:], offs)
+
+        tab_sc = keep.tile([P, T], U8, name="tab_sc", align_bytes=64)
+        nc.vector.memset(tab_sc[:].bitcast(I32), 0)
+        sc_rows = tab_scales.rearrange("a (g e) t -> e g a t", e=2)
+
+        def load_table(words, a, cols):
+            nc.sync.dma_start(words[:, cols].bitcast(I32), tab_words[a, :, cols, :].rearrange("p t i -> p (t i)").bitcast(I32))
+
+        def load_rows(w, a, cols, name):
+            raw = staged([P, PACK, BANK], F32, name)
+            nc.sync.dma_start(raw[:], w[a * PASS : (a + 1) * PASS, cols].rearrange("(p i) c -> p i c", i=PACK))
+            return raw
+
+        def load_w1(a, b):
+            return load_rows(w1, a, slice(b * PASS, (b + 1) * PASS), "w1_raw%d%d" % (a, b))
+
+        tab0 = staged([P, T], U32, "tab0")
+        load_table(tab0, 0, slice(0, T // 2))
+        for e in range(2):
+            nc.sync.dma_start(tab_sc[e:P:PLANE_STEP, :].bitcast(I32), sc_rows[e].bitcast(I32))
+        load_table(tab0, 0, slice(T // 2, T))
+        w1_raw = {(a, 0): load_w1(a, 0) for a in range(2)}
+        tab1 = staged([P, T], U32, "tab1")
+        load_table(tab1, 1, slice(0, T))
+
+        pos1_sb = keep.tile([P, J // 16], U16, name="pos1_sb")
+        nc.sync.dma_start(pos1_sb[:], pos1)
+        pos2_sb = keep.tile([P, J // 16], U16, name="pos2_sb")
+        nc.sync.dma_start(pos2_sb[:], pos2)
+
+        gain_sb = keep.tile([P, 2, PACK], F32, name="gain_sb")
+        nc.gpsimd.dma_start(gain_sb[:], gain.rearrange("(b p t) -> p b t", b=2, t=PACK))
+        rate_sb = keep.tile([P, 2, PACK], F32, name="rate_sb")
+        nc.gpsimd.dma_start(rate_sb[:], rate.rearrange("(b p t) -> p b t", b=2, t=PACK))
+        w3_sc = keep.tile([P, 2, N], U8, name="w3_sc", align_bytes=64)
+        nc.gpsimd.memset(w3_sc[:].bitcast(I32), 0)
+        w3_rows = w3_scales.rearrange("b (d r) n -> r d b n", r=4)
+        for r in range(4):
+            nc.gpsimd.dma_start(w3_sc[r:P:32, :, :].bitcast(I32), w3_rows[r].bitcast(I32))
+
+        picked_sc = keep.tile([P, S], U8, name="picked_sc", align_bytes=64)
+        nc.vector.tensor_copy(picked_sc[:], tab_sc[:].indirect(offs_sb[:]))
+        v_sc = keep.tile([P, S], U8, name="v_sc", align_bytes=64)
+        nc.vector.tensor_copy(v_sc[:].bitcast(I32), picked_sc[:].bitcast(I32))
+        for a in range(2):
+            for e in range(2):
+                row = PLANE_STEP * a + e
+                nc.scalar.dma_start(v_sc[row + 2 : P : 32, :].bitcast(I32), picked_sc[row + 16 : P : 32, :].bitcast(I32))
+
+        def gather_table(words, name):
+            picked = keep.tile([P, S], U32, name=name, align_bytes=64)
+            nc.vector.tensor_copy(picked[:], words[:].indirect(offs_sb[:]))
+            return picked
+
+        def group_w1(a, b, vector_share):
+            grouped = keep.tile([P, PACK, P, PACK], BF16, name="w1_bf%d" % a, tag="w1_bf%d" % a, align_bytes=64)
+            dst = grouped[:].rearrange("p t m i -> p m i t")
+            src = w1_raw[(a, b)][:].rearrange("p i (m t) -> p m i t", t=PACK)
+            if vector_share < P:
+                nc.scalar.copy(dst[:, vector_share:P], src[:, vector_share:P])
+            if vector_share > 0:
+                nc.vector.tensor_copy(dst[:, 0:vector_share], src[:, 0:vector_share])
+            return grouped[:].rearrange("p t m i -> p (t m i)")
+
+        def interleave(copy, planes, name):
+            grouped = keep.tile([P, BANK, PACK], BF16, name=name, align_bytes=64)
+            copy(grouped[:].rearrange("p (c q) i -> p c i q", q=4), planes[:].rearrange("p i (c q) -> p c i q", q=4))
+            return grouped[:].rearrange("p c i -> p (c i)")
+
+        v_codes = [gather_table(tab0, "v_codes0")]
+        w1_mx = {(a, 0): quantize(group_w1(a, 0, W1_VECTOR_SHARE[a]), "w1_%d0" % a) for a in range(2)}
+        v_codes.append(gather_table(tab1, "v_codes1"))
+        for a in range(2):
+            w1_raw[(a, 1)] = load_w1(a, 1)
+        w2_raw = [load_rows(w2, b, slice(0, N), "w2_raw%d" % b) for b in range(2)]
+
+        def first_product(acc, a, b, t, half):
+            codes, scales = w1_mx[(a, b)]
+            rows = slice(t * P, (t + 1) * P)
+            cols = slice(half * BANK, (half + 1) * BANK)
+            nc.tensor.matmul_mx(
+                out=acc[:],
+                lhsT=codes[:, rows].bitcast(FP8X4),
+                lhsT_scale=scales[:, rows],
+                rhs=v_codes[a][:, cols].bitcast(FP8X4),
+                rhs_scale=v_sc[PLANE_STEP * a : P, cols],
+                start=(a == 0),
+                stop=(a == 1),
+            )
+
+        def evacuate(acc, h, b, t, half, on_vector):
+            dst = h[:, half * BANK : (half + 1) * BANK]
+            if on_vector:
+                nc.vector.tensor_scalar(dst, acc[:], gain_sb[:, b, t : t + 1], None, ALU.mult)
+            else:
+                nc.scalar.activation(dst, acc[:], ACT.Copy, scale=gain_sb[:, b, t : t + 1])
+
+        h = {(b, t): keep.tile([P, S], F32, name="h%d%d" % (b, t)) for b in range(2) for t in range(PACK)}
+        x1 = [keep.tile([P, PACK, J], F32, name="x1_%d" % b) for b in range(2)]
+        x2 = [keep.tile([P, PACK, J], F32, name="x2_%d" % b) for b in range(2)]
+
+        def gather_h(x, b, t, pos):
+            nc.vector.tensor_copy(x[b][:, t, :], h[(b, t)][:].indirect(pos[:]))
+
+        def cosine(b, t):
+            angle = x1[b][:, t, :]
+            nc.scalar.activation(angle, angle, ACT.Abs, scale=rate_sb[:, b, t : t + 1])
+            nc.scalar.activation(angle, angle, ACT.Sin, scale=-1.0, bias=math.pi / 2)
+
+        def project(b):
+            grouped = keep.tile([P, J, PACK], BF16, name="z_bf%d" % b, align_bytes=64)
+            nc.vector.tensor_tensor(
+                grouped[:].rearrange("p (c q) t -> p c t q", q=2),
+                x1[b][:].rearrange("p t (c q) -> p c t q", q=2),
+                x2[b][:].rearrange("p t (c q) -> p c t q", q=2),
+                ALU.mult,
+            )
+            return grouped[:].rearrange("p c t -> p (c t)")
+
+        acc = {(t, half): bank(2 * t + half, "h_acc0%d%d" % (t, half)) for t in range(PACK) for half in range(2)}
+        for a in range(2):
+            for t in range(PACK):
+                for half in range(2):
+                    first_product(acc[(t, half)], a, 0, t, half)
+        for t in range(PACK):
+            for half in range(2):
+                evacuate(acc[(t, half)], h[(0, t)], 0, t, half, t == 0 and half == 1)
+            gather_h(x1, 0, t, pos1_sb)
+            gather_h(x2, 0, t, pos2_sb)
+            if t == 1:
+                w1_mx[(0, 1)] = quantize(group_w1(0, 1, 0), "w1_01")
+                w1_mx[(1, 1)] = quantize(group_w1(1, 1, P), "w1_11")
+
+        load_sb = staged([P, N // P, J], F32, "load_sb")
+        nc.sync.dma_start(load_sb[:], load.rearrange("(n p) j -> p n j", p=P))
+        w3_sb = staged([P, 2, 2 * N], U8, "w3_sb")
+        nc.sync.dma_start(w3_sb[:].bitcast(I32), w3_words.rearrange("b p c -> p b c").bitcast(I32))
+
+        for t in range(PACK):
+            for half in range(2):
+                acc1 = bank(2 * t + half, "h_acc1%d%d" % (t, half))
+                for a in range(2):
+                    first_product(acc1, a, 1, t, half)
+                evacuate(acc1, h[(1, t)], 1, t, half, False)
+        for t in range(PACK):
+            gather_h(x1, 1, t, pos1_sb)
+        for t in range(PACK):
+            cosine(0, t)
+        w2_mx = [quantize(interleave(nc.scalar.copy, w2_raw[0], "w2_bf0"), "w2_0")]
+
+        turned = [bank(n, "turned%d" % n) for n in range(N // P)]
+        direct = [bank(N // P + n, "direct%d" % n) for n in range(N // P)]
+
+        def second_products(b):
+            x2_bf = interleave(nc.scalar.copy, x2[b], "x2_bf%d" % b)
+            z_codes, z_scales = quantize(project(b), "z%d" % b)
+            x2_codes, x2_scales = quantize(x2_bf, "x2_%d" % b)
+            w2_codes, w2_scales = w2_mx[b]
+            for n in range(N // P):
+                cols = slice(n * P, (n + 1) * P)
+                nc.tensor.matmul_mx(
+                    out=turned[n][:],
+                    lhsT=w2_codes[:, cols].bitcast(FP8X4),
+                    lhsT_scale=w2_scales[:, cols],
+                    rhs=z_codes[:].bitcast(FP8X4),
+                    rhs_scale=z_scales[:],
+                    start=(b == 0),
+                    stop=(b == 1),
+                )
+            for n in range(N // P):
+                nc.tensor.matmul_mx(
+                    out=direct[n][:],
+                    lhsT=w3_sb[:, b, 2 * n * P : 2 * (n + 1) * P].bitcast(FP4X4),
+                    lhsT_scale=w3_sc[:, b, n * P : (n + 1) * P],
+                    rhs=x2_codes[:].bitcast(FP8X4),
+                    rhs_scale=x2_scales[:],
+                    start=(b == 0),
+                    stop=(b == 1),
+                )
+
+        second_products(0)
+        for t in range(PACK):
+            cosine(1, t)
+        w2_mx.append(quantize(interleave(nc.scalar.copy, w2_raw[1], "w2_bf1"), "w2_1"))
+        for t in range(PACK):
+            gather_h(x2, 1, t, pos2_sb)
+        second_products(1)
+
+        weighted = [keep.tile([P, J], F32, name="weighted%d" % n) for n in range(N // P)]
+        result = [keep.tile([P, J], F32, name="result%d" % n) for n in range(N // P)]
+        for n in range(N // P + 1):
+            if n < N // P:
+                nc.vector.tensor_tensor(weighted[n][:], turned[n][:], load_sb[:, n, :], ALU.mult)
+            if n > 0:
+                nc.vector.tensor_tensor(result[n - 1][:], direct[n - 1][:], weighted[n - 1][:], ALU.add)
+                nc.sync.dma_start(out[(n - 1) * P : n * P, :], result[n - 1][:])

@@ -22,6 +22,7 @@ PACK = 4
 PASS = P * PACK
 BANK = 512
 PLANE_STEP = 8
+GPSIMD_COLUMNS = 256
 W1_VECTOR_SHARE = (32, 64)
 
 
@@ -56,6 +57,10 @@ def tile_list_aligner_stage_forces_kernel(
         tab_sc = keep.tile([P, T], U8, name="tab_sc", align_bytes=64)
         nc.vector.memset(tab_sc[:].bitcast(I32), 0)
         sc_rows = tab_scales.rearrange("a (g e) t -> e g a t", e=2)
+
+        warm = keep.tile([P, 1], F32, name="warm")
+        nc.gpsimd.memset(warm[:], 0.0)
+        nc.scalar.activation(warm[:], warm[:], ACT.Sin)
 
         def load_table(words, a, cols):
             nc.sync.dma_start(words[:, cols].bitcast(I32), tab_words[a, :, cols, :].rearrange("p t i -> p (t i)").bitcast(I32))
@@ -121,6 +126,15 @@ def tile_list_aligner_stage_forces_kernel(
             copy(grouped[:].rearrange("p (c q) i -> p c i q", q=4), planes[:].rearrange("p i (c q) -> p c i q", q=4))
             return grouped[:].rearrange("p c i -> p (c i)")
 
+        def interleave_on_gpsimd(planes, name):
+            grouped = keep.tile([P, BANK, PACK], BF16, name=name, align_bytes=64)
+            for c in range(0, BANK, GPSIMD_COLUMNS):
+                cols = slice(c, c + GPSIMD_COLUMNS)
+                nc.gpsimd.tensor_scalar(
+                    grouped[:, cols, :], planes[:, :, cols].rearrange("p i c -> p c i"), 1.0, 0.0, ALU.mult, ALU.add
+                )
+            return grouped[:].rearrange("p c i -> p (c i)")
+
         v_codes = [gather_table(tab0, "v_codes0")]
         w1_mx = {(a, 0): quantize(group_w1(a, 0, W1_VECTOR_SHARE[a]), "w1_%d0" % a) for a in range(2)}
         v_codes.append(gather_table(tab1, "v_codes1"))
@@ -150,67 +164,77 @@ def tile_list_aligner_stage_forces_kernel(
                 nc.scalar.activation(dst, acc[:], ACT.Copy, scale=gain_sb[:, b, t : t + 1])
 
         h = {(b, t): keep.tile([P, S], F32, name="h%d%d" % (b, t)) for b in range(2) for t in range(PACK)}
-        x1 = [keep.tile([P, PACK, J], F32, name="x1_%d" % b) for b in range(2)]
+        cos = [keep.tile([P, PACK, J], F32, name="cos%d" % b) for b in range(2)]
+        x1 = {}
         x2 = [keep.tile([P, PACK, J], F32, name="x2_%d" % b) for b in range(2)]
 
-        def gather_h(x, b, t, pos):
-            nc.vector.tensor_copy(x[b][:, t, :], h[(b, t)][:].indirect(pos[:]))
+        def gather_h(b, t):
+            tag = "w1_bf%d" % (t - 2) if b == 0 and t >= 2 else "x1_%d%d" % (b, t)
+            x1[(b, t)] = keep.tile([P, J], F32, name="x1_%d%d" % (b, t), tag=tag, align_bytes=64)
+            nc.vector.tensor_copy(x1[(b, t)][:], h[(b, t)][:].indirect(pos1_sb[:]))
+            nc.vector.tensor_copy(x2[b][:, t, :], h[(b, t)][:].indirect(pos2_sb[:]))
 
         def cosine(b, t):
-            angle = x1[b][:, t, :]
+            angle = x1[(b, t)][:]
             nc.scalar.activation(angle, angle, ACT.Abs, scale=rate_sb[:, b, t : t + 1])
-            nc.scalar.activation(angle, angle, ACT.Sin, scale=-1.0, bias=math.pi / 2)
+            nc.scalar.activation(cos[b][:, t, :], angle, ACT.Sin, scale=-1.0, bias=math.pi / 2)
 
         def project(b):
             grouped = keep.tile([P, J, PACK], BF16, name="z_bf%d" % b, align_bytes=64)
-            nc.vector.tensor_tensor(
-                grouped[:].rearrange("p (c q) t -> p c t q", q=2),
-                x1[b][:].rearrange("p t (c q) -> p c t q", q=2),
-                x2[b][:].rearrange("p t (c q) -> p c t q", q=2),
-                ALU.mult,
-            )
+            step = GPSIMD_COLUMNS if b == 0 else J
+            for c in range(0, J, step):
+                cols = slice(c, c + step)
+                (nc.gpsimd if b == 0 else nc.vector).tensor_tensor(
+                    grouped[:, cols, :].rearrange("p (c q) t -> p c t q", q=2),
+                    cos[b][:, :, cols].rearrange("p t (c q) -> p c t q", q=2),
+                    x2[b][:, :, cols].rearrange("p t (c q) -> p c t q", q=2),
+                    ALU.mult,
+                )
             return grouped[:].rearrange("p c t -> p (c t)")
 
-        acc = {(t, half): bank(2 * t + half, "h_acc0%d%d" % (t, half)) for t in range(PACK) for half in range(2)}
-        for a in range(2):
-            for t in range(PACK):
-                for half in range(2):
-                    first_product(acc[(t, half)], a, 0, t, half)
-        for t in range(PACK):
+        def h_slice(b, t, passes):
             for half in range(2):
-                evacuate(acc[(t, half)], h[(0, t)], 0, t, half, t == 0 and half == 1)
-            gather_h(x1, 0, t, pos1_sb)
-            gather_h(x2, 0, t, pos2_sb)
-            if t == 1:
-                w1_mx[(0, 1)] = quantize(group_w1(0, 1, 0), "w1_01")
-                w1_mx[(1, 1)] = quantize(group_w1(1, 1, P), "w1_11")
+                if (b, t, half) not in acc:
+                    acc[(b, t, half)] = bank(2 * (t % 2) + half, "h_acc%d%d%d" % (b, t, half))
+                for a in passes:
+                    first_product(acc[(b, t, half)], a, b, t, half)
+
+        acc = {}
+        for t in range(2):
+            h_slice(0, t, [0])
+        for t in range(PACK):
+            h_slice(0, t, [1] if t < 2 else [0, 1])
+            for half in range(2):
+                evacuate(acc[(0, t, half)], h[(0, t)], 0, t, half, t == 0 and half == 1)
+            gather_h(0, t)
+            if t in (1, 2):
+                w1_mx[(t - 1, 1)] = quantize(group_w1(t - 1, 1, 0), "w1_%d1" % (t - 1))
 
         load_sb = staged([P, N // P, J], F32, "load_sb")
         nc.sync.dma_start(load_sb[:], load.rearrange("(n p) j -> p n j", p=P))
         w3_sb = staged([P, 2, 2 * N], U8, "w3_sb")
         nc.sync.dma_start(w3_sb[:].bitcast(I32), w3_words.rearrange("b p c -> p b c").bitcast(I32))
 
+        cosine(0, 0)
         for t in range(PACK):
+            h_slice(1, t, [0, 1])
             for half in range(2):
-                acc1 = bank(2 * t + half, "h_acc1%d%d" % (t, half))
-                for a in range(2):
-                    first_product(acc1, a, 1, t, half)
-                evacuate(acc1, h[(1, t)], 1, t, half, False)
-        for t in range(PACK):
-            gather_h(x1, 1, t, pos1_sb)
-        for t in range(PACK):
-            cosine(0, t)
-        w2_mx = [quantize(interleave(nc.scalar.copy, w2_raw[0], "w2_bf0"), "w2_0")]
+                evacuate(acc[(1, t, half)], h[(1, t)], 1, t, half, False)
+            if t + 1 < PACK:
+                cosine(0, t + 1)
+            gather_h(1, t)
+        w2_mx = [quantize(interleave_on_gpsimd(w2_raw[b], "w2_bf%d" % b), "w2_%d" % b) for b in range(2)]
 
-        turned = [bank(n, "turned%d" % n) for n in range(N // P)]
-        direct = [bank(N // P + n, "direct%d" % n) for n in range(N // P)]
+        turned = [bank(N // P + n, "turned%d" % n) for n in range(N // P)]
+        direct = [bank(n, "direct%d" % n) for n in range(N // P)]
 
         def second_products(b):
-            x2_bf = interleave(nc.scalar.copy, x2[b], "x2_bf%d" % b)
+            x2_bf = interleave(nc.scalar.copy, x2[b], "x2_bf1") if b == 1 else interleave_on_gpsimd(x2[b], "x2_bf0")
             z_codes, z_scales = quantize(project(b), "z%d" % b)
             x2_codes, x2_scales = quantize(x2_bf, "x2_%d" % b)
             w2_codes, w2_scales = w2_mx[b]
-            for n in range(N // P):
+
+            def turn(n):
                 cols = slice(n * P, (n + 1) * P)
                 nc.tensor.matmul_mx(
                     out=turned[n][:],
@@ -221,7 +245,8 @@ def tile_list_aligner_stage_forces_kernel(
                     start=(b == 0),
                     stop=(b == 1),
                 )
-            for n in range(N // P):
+
+            def read_direct(n):
                 nc.tensor.matmul_mx(
                     out=direct[n][:],
                     lhsT=w3_sb[:, b, 2 * n * P : 2 * (n + 1) * P].bitcast(FP4X4),
@@ -232,12 +257,15 @@ def tile_list_aligner_stage_forces_kernel(
                     stop=(b == 1),
                 )
 
+            turn(0)
+            for n in range(N // P):
+                read_direct(n)
+                if n + 1 < N // P:
+                    turn(n + 1)
+
         second_products(0)
         for t in range(PACK):
             cosine(1, t)
-        w2_mx.append(quantize(interleave(nc.scalar.copy, w2_raw[1], "w2_bf1"), "w2_1"))
-        for t in range(PACK):
-            gather_h(x2, 1, t, pos2_sb)
         second_products(1)
 
         weighted = [keep.tile([P, J], F32, name="weighted%d" % n) for n in range(N // P)]

@@ -22,7 +22,7 @@ PACK = 4
 PASS = P * PACK
 BANK = 512
 PLANE_STEP = 8
-GPSIMD_COLUMNS = 256
+GPSIMD_COLUMNS = 128
 W1_VECTOR_SHARE = (32, 64)
 
 
@@ -32,22 +32,22 @@ def tile_list_aligner_stage_forces_kernel(
     nc = tc.nc
     with ExitStack() as ctx:
         keep = ctx.enter_context(tc.tile_pool(name="keep", bufs=1))
-        stage = ctx.enter_context(tc.tile_pool(name="stage", bufs=4))
+        stage = ctx.enter_context(tc.tile_pool(name="stage", bufs=1))
         psum = ctx.enter_context(tc.psum_pool(name="psum", bufs=1))
 
         def bank(i, name):
             return psum.tile([P, BANK], F32, name=name, tag="bank%d" % i)
 
-        def staged(shape, dtype, name):
-            return stage.tile(shape, dtype, name=name, tag="stage", align_bytes=64)
+        def staged(slot, shape, dtype, name):
+            return stage.tile(shape, dtype, name=name, tag="slot%d" % slot, align_bytes=64)
 
-        def mx_tiles(name, width):
-            codes = keep.tile([P, width], U32, name=name + "_codes", align_bytes=64)
+        def mx_tiles(name, width, tag):
+            codes = keep.tile([P, width], U32, name=name + "_codes", tag=tag, align_bytes=64)
             scales = keep.tile([P, width], U8, name=name + "_scales", align_bytes=64)
             return codes, scales
 
-        def quantize(grouped, name):
-            codes, scales = mx_tiles(name, BANK)
+        def quantize(grouped, name, tag=""):
+            codes, scales = mx_tiles(name, grouped.shape[1] // PACK, tag or name + "_codes")
             nc.vector.quantize_mx(out=codes[:].bitcast(FP8X4), scales=scales[:], in_=grouped)
             return codes, scales
 
@@ -65,21 +65,21 @@ def tile_list_aligner_stage_forces_kernel(
         def load_table(words, a, cols):
             nc.sync.dma_start(words[:, cols].bitcast(I32), tab_words[a, :, cols, :].rearrange("p t i -> p (t i)").bitcast(I32))
 
-        def load_rows(w, a, cols, name):
-            raw = staged([P, PACK, BANK], F32, name)
+        def load_rows(slot, w, a, cols, name):
+            raw = staged(slot, [P, PACK, BANK], F32, name)
             nc.sync.dma_start(raw[:], w[a * PASS : (a + 1) * PASS, cols].rearrange("(p i) c -> p i c", i=PACK))
             return raw
 
         def load_w1(a, b):
-            return load_rows(w1, a, slice(b * PASS, (b + 1) * PASS), "w1_raw%d%d" % (a, b))
+            return load_rows(a + 1 - b, w1, a, slice(b * PASS, (b + 1) * PASS), "w1_raw%d%d" % (a, b))
 
-        tab0 = staged([P, T], U32, "tab0")
+        tab0 = staged(0, [P, T], U32, "tab0")
         load_table(tab0, 0, slice(0, T // 2))
         for e in range(2):
             nc.sync.dma_start(tab_sc[e:P:PLANE_STEP, :].bitcast(I32), sc_rows[e].bitcast(I32))
         load_table(tab0, 0, slice(T // 2, T))
         w1_raw = {(a, 0): load_w1(a, 0) for a in range(2)}
-        tab1 = staged([P, T], U32, "tab1")
+        tab1 = staged(3, [P, T], U32, "tab1")
         load_table(tab1, 1, slice(0, T))
 
         pos1_sb = keep.tile([P, J // 16], U16, name="pos1_sb")
@@ -106,13 +106,15 @@ def tile_list_aligner_stage_forces_kernel(
                 row = PLANE_STEP * a + e
                 nc.scalar.dma_start(v_sc[row + 2 : P : 32, :].bitcast(I32), picked_sc[row + 16 : P : 32, :].bitcast(I32))
 
-        def gather_table(words, name):
-            picked = keep.tile([P, S], U32, name=name, align_bytes=64)
-            nc.vector.tensor_copy(picked[:], words[:].indirect(offs_sb[:]))
+        def gather_table(words, name, step):
+            picked = keep.tile([P, S], U32, name=name, tag=name, align_bytes=64)
+            for m in range(0, S, step):
+                nc.vector.tensor_copy(picked[:, m : m + step], words[:].indirect(offs_sb[:, m // 16 : (m + step) // 16]))
             return picked
 
         def group_w1(a, b, vector_share):
-            grouped = keep.tile([P, PACK, P, PACK], BF16, name="w1_bf%d" % a, tag="w1_bf%d" % a, align_bytes=64)
+            tag = "v_codes1" if (a, b) == (1, 0) else "w1_bf%d" % a
+            grouped = keep.tile([P, PACK, P, PACK], BF16, name="w1_bf%d%d" % (a, b), tag=tag, align_bytes=64)
             dst = grouped[:].rearrange("p t m i -> p m i t")
             src = w1_raw[(a, b)][:].rearrange("p i (m t) -> p m i t", t=PACK)
             if vector_share < P:
@@ -126,21 +128,19 @@ def tile_list_aligner_stage_forces_kernel(
             copy(grouped[:].rearrange("p (c q) i -> p c i q", q=4), planes[:].rearrange("p i (c q) -> p c i q", q=4))
             return grouped[:].rearrange("p c i -> p (c i)")
 
-        def interleave_on_gpsimd(planes, name):
-            grouped = keep.tile([P, BANK, PACK], BF16, name=name, align_bytes=64)
+        def interleave_on_gpsimd(planes, grouped):
             for c in range(0, BANK, GPSIMD_COLUMNS):
                 cols = slice(c, c + GPSIMD_COLUMNS)
                 nc.gpsimd.tensor_scalar(
                     grouped[:, cols, :], planes[:, :, cols].rearrange("p i c -> p c i"), 1.0, 0.0, ALU.mult, ALU.add
                 )
-            return grouped[:].rearrange("p c i -> p (c i)")
 
-        v_codes = [gather_table(tab0, "v_codes0")]
+        v_codes = [gather_table(tab0, "v_codes0", S)]
         w1_mx = {(a, 0): quantize(group_w1(a, 0, W1_VECTOR_SHARE[a]), "w1_%d0" % a) for a in range(2)}
-        v_codes.append(gather_table(tab1, "v_codes1"))
+        v_codes.append(gather_table(tab1, "v_codes1", BANK))
         for a in range(2):
             w1_raw[(a, 1)] = load_w1(a, 1)
-        w2_raw = [load_rows(w2, b, slice(0, N), "w2_raw%d" % b) for b in range(2)]
+        w2_raw = [load_rows(2 + b, w2, b, slice(0, N), "w2_raw%d" % b) for b in range(2)]
 
         def first_product(acc, a, b, t, half):
             codes, scales = w1_mx[(a, b)]
@@ -169,7 +169,7 @@ def tile_list_aligner_stage_forces_kernel(
         x2 = [keep.tile([P, PACK, J], F32, name="x2_%d" % b) for b in range(2)]
 
         def gather_h(b, t):
-            tag = "w1_bf%d" % (t - 2) if b == 0 and t >= 2 else "x1_%d%d" % (b, t)
+            tag = {(0, 2): "w1_bf0", (0, 3): "w1_bf1", (1, 0): "w2_bf"}.get((b, t), "x1_%d%d" % (b, t))
             x1[(b, t)] = keep.tile([P, J], F32, name="x1_%d%d" % (b, t), tag=tag, align_bytes=64)
             nc.vector.tensor_copy(x1[(b, t)][:], h[(b, t)][:].indirect(pos1_sb[:]))
             nc.vector.tensor_copy(x2[b][:, t, :], h[(b, t)][:].indirect(pos2_sb[:]))
@@ -179,9 +179,8 @@ def tile_list_aligner_stage_forces_kernel(
             nc.scalar.activation(angle, angle, ACT.Abs, scale=rate_sb[:, b, t : t + 1])
             nc.scalar.activation(cos[b][:, t, :], angle, ACT.Sin, scale=-1.0, bias=math.pi / 2)
 
-        def project(b):
-            grouped = keep.tile([P, J, PACK], BF16, name="z_bf%d" % b, align_bytes=64)
-            step = GPSIMD_COLUMNS if b == 0 else J
+        def project(b, grouped):
+            step = J // 2 if b == 0 else J
             for c in range(0, J, step):
                 cols = slice(c, c + step)
                 (nc.gpsimd if b == 0 else nc.vector).tensor_tensor(
@@ -190,7 +189,6 @@ def tile_list_aligner_stage_forces_kernel(
                     x2[b][:, :, cols].rearrange("p t (c q) -> p c t q", q=2),
                     ALU.mult,
                 )
-            return grouped[:].rearrange("p c t -> p (c t)")
 
         def h_slice(b, t, passes):
             for half in range(2):
@@ -210,38 +208,38 @@ def tile_list_aligner_stage_forces_kernel(
             if t in (1, 2):
                 w1_mx[(t - 1, 1)] = quantize(group_w1(t - 1, 1, 0), "w1_%d1" % (t - 1))
 
-        load_sb = staged([P, N // P, J], F32, "load_sb")
+        load_sb = staged(0, [P, N // P, J], F32, "load_sb")
         nc.sync.dma_start(load_sb[:], load.rearrange("(n p) j -> p n j", p=P))
-        w3_sb = staged([P, 2, 2 * N], U8, "w3_sb")
+        w3_sb = staged(1, [P, 2, 2 * N], U8, "w3_sb")
         nc.sync.dma_start(w3_sb[:].bitcast(I32), w3_words.rearrange("b p c -> p b c").bitcast(I32))
 
+        w2_bf = keep.tile([P, 2, N, PACK], BF16, name="w2_bf", tag="w2_bf", align_bytes=64)
+        for b in range(2):
+            interleave_on_gpsimd(w2_raw[b], w2_bf[:, b])
+        w2_codes, w2_scales = quantize(w2_bf[:].rearrange("p b n i -> p (b n i)"), "w2")
+
         cosine(0, 0)
+        cosine(0, 1)
         for t in range(PACK):
             h_slice(1, t, [0, 1])
             for half in range(2):
                 evacuate(acc[(1, t, half)], h[(1, t)], 1, t, half, False)
-            if t + 1 < PACK:
-                cosine(0, t + 1)
+            if t < 2:
+                cosine(0, t + 2)
             gather_h(1, t)
-        w2_mx = [quantize(interleave_on_gpsimd(w2_raw[b], "w2_bf%d" % b), "w2_%d" % b) for b in range(2)]
 
         turned = [bank(N // P + n, "turned%d" % n) for n in range(N // P)]
         direct = [bank(n, "direct%d" % n) for n in range(N // P)]
 
-        def second_products(b):
-            x2_bf = interleave(nc.scalar.copy, x2[b], "x2_bf1") if b == 1 else interleave_on_gpsimd(x2[b], "x2_bf0")
-            z_codes, z_scales = quantize(project(b), "z%d" % b)
-            x2_codes, x2_scales = quantize(x2_bf, "x2_%d" % b)
-            w2_codes, w2_scales = w2_mx[b]
-
+        def second_products(b, z_codes, z_scales, x2_codes, x2_scales):
             def turn(n):
-                cols = slice(n * P, (n + 1) * P)
+                cols = slice(b * N + n * P, b * N + (n + 1) * P)
                 nc.tensor.matmul_mx(
                     out=turned[n][:],
                     lhsT=w2_codes[:, cols].bitcast(FP8X4),
                     lhsT_scale=w2_scales[:, cols],
-                    rhs=z_codes[:].bitcast(FP8X4),
-                    rhs_scale=z_scales[:],
+                    rhs=z_codes.bitcast(FP8X4),
+                    rhs_scale=z_scales,
                     start=(b == 0),
                     stop=(b == 1),
                 )
@@ -251,22 +249,30 @@ def tile_list_aligner_stage_forces_kernel(
                     out=direct[n][:],
                     lhsT=w3_sb[:, b, 2 * n * P : 2 * (n + 1) * P].bitcast(FP4X4),
                     lhsT_scale=w3_sc[:, b, n * P : (n + 1) * P],
-                    rhs=x2_codes[:].bitcast(FP8X4),
-                    rhs_scale=x2_scales[:],
+                    rhs=x2_codes.bitcast(FP8X4),
+                    rhs_scale=x2_scales,
                     start=(b == 0),
                     stop=(b == 1),
                 )
 
-            turn(0)
             for n in range(N // P):
+                turn(n)
                 read_direct(n)
-                if n + 1 < N // P:
-                    turn(n + 1)
 
-        second_products(0)
+        pair_bf = keep.tile([P, 2, J, PACK], BF16, name="pair_bf", align_bytes=64)
+        interleave_on_gpsimd(x2[0], pair_bf[:, 0])
+        project(0, pair_bf[:, 1])
+        codes, scales = quantize(pair_bf[:].rearrange("p s j t -> p (s j t)"), "pair0")
+        second_products(0, codes[:, J : 2 * J], scales[:, J : 2 * J], codes[:, 0:J], scales[:, 0:J])
+
         for t in range(PACK):
             cosine(1, t)
-        second_products(1)
+        x2_bf = interleave(nc.scalar.copy, x2[1], "x2_bf1")
+        z_bf = keep.tile([P, J, PACK], BF16, name="z_bf1", tag="z_bf1", align_bytes=64)
+        project(1, z_bf)
+        z_codes, z_scales = quantize(z_bf[:].rearrange("p j t -> p (j t)"), "z1")
+        x2_codes, x2_scales = quantize(x2_bf, "x2_1", "z_bf1")
+        second_products(1, z_codes[:], z_scales[:], x2_codes[:], x2_scales[:])
 
         weighted = [keep.tile([P, J], F32, name="weighted%d" % n) for n in range(N // P)]
         result = [keep.tile([P, J], F32, name="result%d" % n) for n in range(N // P)]

@@ -22,7 +22,7 @@ PACK = 4
 PASS = P * PACK
 BANK = 512
 PLANE_STEP = 8
-GPSIMD_COLUMNS = 128
+GPSIMD_COLUMNS = 512
 W1_VECTOR_SHARE = (32, 64)
 
 
@@ -33,6 +33,7 @@ def tile_list_aligner_stage_forces_kernel(
     with ExitStack() as ctx:
         keep = ctx.enter_context(tc.tile_pool(name="keep", bufs=1))
         stage = ctx.enter_context(tc.tile_pool(name="stage", bufs=1))
+        lent = ctx.enter_context(tc.tile_pool(name="lent", bufs=1))
         psum = ctx.enter_context(tc.psum_pool(name="psum", bufs=1))
 
         def bank(i, name):
@@ -58,8 +59,8 @@ def tile_list_aligner_stage_forces_kernel(
         nc.vector.memset(tab_sc[:].bitcast(I32), 0)
         sc_rows = tab_scales.rearrange("a (g e) t -> e g a t", e=2)
 
-        warm = keep.tile([P, 1], F32, name="warm")
-        nc.gpsimd.memset(warm[:], 0.0)
+        warm = lent.tile([P, 4 * PACK], F32, name="warm", offset=24 * J)
+        nc.vector.memset(warm[:], 0.0)
         nc.scalar.activation(warm[:], warm[:], ACT.Sin)
 
         def load_table(words, a, cols):
@@ -87,12 +88,12 @@ def tile_list_aligner_stage_forces_kernel(
         pos2_sb = keep.tile([P, J // 16], U16, name="pos2_sb")
         nc.sync.dma_start(pos2_sb[:], pos2)
 
-        gain_sb = keep.tile([P, 2, PACK], F32, name="gain_sb")
+        gain_sb = lent.tile([P, 2, PACK], F32, name="gain_sb", offset=24 * J)
         nc.gpsimd.dma_start(gain_sb[:], gain.rearrange("(b p t) -> p b t", b=2, t=PACK))
-        rate_sb = keep.tile([P, 2, PACK], F32, name="rate_sb")
+        rate_sb = lent.tile([P, 2, PACK], F32, name="rate_sb", offset=24 * J + 32)
         nc.gpsimd.dma_start(rate_sb[:], rate.rearrange("(b p t) -> p b t", b=2, t=PACK))
         w3_sc = keep.tile([P, 2, N], U8, name="w3_sc", align_bytes=64)
-        nc.gpsimd.memset(w3_sc[:].bitcast(I32), 0)
+        nc.vector.memset(w3_sc[:].bitcast(I32), 0)
         w3_rows = w3_scales.rearrange("b (d r) n -> r d b n", r=4)
         for r in range(4):
             nc.gpsimd.dma_start(w3_sc[r:P:32, :, :].bitcast(I32), w3_rows[r].bitcast(I32))
@@ -113,8 +114,11 @@ def tile_list_aligner_stage_forces_kernel(
             return picked
 
         def group_w1(a, b, vector_share):
-            tag = "v_codes1" if (a, b) == (1, 0) else "w1_bf%d" % a
-            grouped = keep.tile([P, PACK, P, PACK], BF16, name="w1_bf%d%d" % (a, b), tag=tag, align_bytes=64)
+            if (a, b) == (1, 1):
+                grouped = lent.tile([P, PACK, P, PACK], BF16, name="w1_bf11", align_bytes=64, offset=4 * J)
+            else:
+                tag = "v_codes1" if a == 1 else "w1_bf0"
+                grouped = keep.tile([P, PACK, P, PACK], BF16, name="w1_bf%d%d" % (a, b), tag=tag, align_bytes=64)
             dst = grouped[:].rearrange("p t m i -> p m i t")
             src = w1_raw[(a, b)][:].rearrange("p i (m t) -> p m i t", t=PACK)
             if vector_share < P:
@@ -123,10 +127,8 @@ def tile_list_aligner_stage_forces_kernel(
                 nc.vector.tensor_copy(dst[:, 0:vector_share], src[:, 0:vector_share])
             return grouped[:].rearrange("p t m i -> p (t m i)")
 
-        def interleave(copy, planes, name):
-            grouped = keep.tile([P, BANK, PACK], BF16, name=name, align_bytes=64)
-            copy(grouped[:].rearrange("p (c q) i -> p c i q", q=4), planes[:].rearrange("p i (c q) -> p c i q", q=4))
-            return grouped[:].rearrange("p c i -> p (c i)")
+        def interleave(planes, grouped):
+            nc.scalar.copy(grouped.rearrange("p (c q) i -> p c i q", q=4), planes[:].rearrange("p i (c q) -> p c i q", q=4))
 
         def interleave_on_gpsimd(planes, grouped):
             for c in range(0, BANK, GPSIMD_COLUMNS):
@@ -163,14 +165,17 @@ def tile_list_aligner_stage_forces_kernel(
             else:
                 nc.scalar.activation(dst, acc[:], ACT.Copy, scale=gain_sb[:, b, t : t + 1])
 
-        h = {(b, t): keep.tile([P, S], F32, name="h%d%d" % (b, t)) for b in range(2) for t in range(PACK)}
+        h = {(b, t): keep.tile([P, S], F32, name="h%d%d" % (b, t), tag="h%d%d" % (b, t), align_bytes=64) for b in range(2) for t in range(PACK) if (b, t) != (1, 2)}
         cos = [keep.tile([P, PACK, J], F32, name="cos%d" % b) for b in range(2)]
         x1 = {}
         x2 = [keep.tile([P, PACK, J], F32, name="x2_%d" % b) for b in range(2)]
 
         def gather_h(b, t):
-            tag = {(0, 2): "w1_bf0", (0, 3): "w1_bf1", (1, 0): "w2_bf"}.get((b, t), "x1_%d%d" % (b, t))
-            x1[(b, t)] = keep.tile([P, J], F32, name="x1_%d%d" % (b, t), tag=tag, align_bytes=64)
+            if (b, t) == (0, 3):
+                x1[(b, t)] = lent.tile([P, J], F32, name="x1_03", align_bytes=64, offset=4 * J)
+            else:
+                tag = "w1_bf0" if (b, t) == (0, 2) else "x1_%d%d" % (b, t)
+                x1[(b, t)] = keep.tile([P, J], F32, name="x1_%d%d" % (b, t), tag=tag, align_bytes=64)
             nc.vector.tensor_copy(x1[(b, t)][:], h[(b, t)][:].indirect(pos1_sb[:]))
             nc.vector.tensor_copy(x2[b][:, t, :], h[(b, t)][:].indirect(pos2_sb[:]))
 
@@ -180,7 +185,7 @@ def tile_list_aligner_stage_forces_kernel(
             nc.scalar.activation(cos[b][:, t, :], angle, ACT.Sin, scale=-1.0, bias=math.pi / 2)
 
         def project(b, grouped):
-            step = J // 2 if b == 0 else J
+            step = J
             for c in range(0, J, step):
                 cols = slice(c, c + step)
                 (nc.gpsimd if b == 0 else nc.vector).tensor_tensor(
@@ -213,11 +218,11 @@ def tile_list_aligner_stage_forces_kernel(
         w3_sb = staged(1, [P, 2, 2 * N], U8, "w3_sb")
         nc.sync.dma_start(w3_sb[:].bitcast(I32), w3_words.rearrange("b p c -> p b c").bitcast(I32))
 
-        w2_bf = keep.tile([P, 2, N, PACK], BF16, name="w2_bf", tag="w2_bf", align_bytes=64)
+        w2_bf = lent.tile([P, 2, N, PACK], BF16, name="w2_bf", align_bytes=64, offset=8 * J)
         for b in range(2):
             interleave_on_gpsimd(w2_raw[b], w2_bf[:, b])
-        w2_codes, w2_scales = quantize(w2_bf[:].rearrange("p b n i -> p (b n i)"), "w2")
 
+        h[(1, 2)] = lent.tile([P, S], F32, name="h12", align_bytes=64, offset=0)
         cosine(0, 0)
         cosine(0, 1)
         for t in range(PACK):
@@ -228,6 +233,7 @@ def tile_list_aligner_stage_forces_kernel(
                 cosine(0, t + 2)
             gather_h(1, t)
 
+        w2_codes, w2_scales = quantize(w2_bf[:].rearrange("p b n i -> p (b n i)"), "w2", "h13")
         turned = [bank(N // P + n, "turned%d" % n) for n in range(N // P)]
         direct = [bank(n, "direct%d" % n) for n in range(N // P)]
 
@@ -260,18 +266,19 @@ def tile_list_aligner_stage_forces_kernel(
                 read_direct(n)
 
         pair_bf = keep.tile([P, 2, J, PACK], BF16, name="pair_bf", align_bytes=64)
-        interleave_on_gpsimd(x2[0], pair_bf[:, 0])
+        interleave(x2[0], pair_bf[:, 0])
         project(0, pair_bf[:, 1])
         codes, scales = quantize(pair_bf[:].rearrange("p s j t -> p (s j t)"), "pair0")
         second_products(0, codes[:, J : 2 * J], scales[:, J : 2 * J], codes[:, 0:J], scales[:, 0:J])
 
         for t in range(PACK):
             cosine(1, t)
-        x2_bf = interleave(nc.scalar.copy, x2[1], "x2_bf1")
+        x2_bf = keep.tile([P, J, PACK], BF16, name="x2_bf1", align_bytes=64)
+        interleave(x2[1], x2_bf[:])
         z_bf = keep.tile([P, J, PACK], BF16, name="z_bf1", tag="z_bf1", align_bytes=64)
         project(1, z_bf)
         z_codes, z_scales = quantize(z_bf[:].rearrange("p j t -> p (j t)"), "z1")
-        x2_codes, x2_scales = quantize(x2_bf, "x2_1", "z_bf1")
+        x2_codes, x2_scales = quantize(x2_bf[:].rearrange("p j t -> p (j t)"), "x2_1", "z_bf1")
         second_products(1, z_codes[:], z_scales[:], x2_codes[:], x2_scales[:])
 
         weighted = [keep.tile([P, J], F32, name="weighted%d" % n) for n in range(N // P)]

import math
from contextlib import ExitStack

import concourse.mybir as mybir

K, H, N, T, S, J = 1024, 1024, 512, 2048, 1024, 512
FLOPS = 2 * K * H * S + 2 * 2 * H * N * J

F32 = mybir.dt.float32
BF16 = mybir.dt.bfloat16
I32 = mybir.dt.int32
U32 = mybir.dt.uint32
U16 = mybir.dt.uint16
U8 = mybir.dt.uint8
FP8X4 = mybir.dt.float8_e4m3fn_x4
FP4X4 = mybir.dt.float4_e2m1fn_x4
ACT = mybir.ActivationFunctionType
ALU = mybir.AluOpType

P = 128
PACK = 4
PASS = P * PACK
BANK = 512
PLANE_STEP = 8
GPSIMD_COLUMNS = 512
W1_VECTOR_SHARE = (32, 64)


def tile_list_aligner_stage_forces_kernel(
    tc, tab_words, tab_scales, offs, pos1, pos2, w1, gain, rate, w2, w3_words, w3_scales, load, out
):
    nc = tc.nc
    with ExitStack() as ctx:
        keep = ctx.enter_context(tc.tile_pool(name="keep", bufs=1))
        stage = ctx.enter_context(tc.tile_pool(name="stage", bufs=1))
        lent = ctx.enter_context(tc.tile_pool(name="lent", bufs=1))
        psum = ctx.enter_context(tc.psum_pool(name="psum", bufs=1))

        def bank(i, name):
            return psum.tile([P, BANK], F32, name=name, tag="bank%d" % i)

        def staged(slot, shape, dtype, name):
            return stage.tile(shape, dtype, name=name, tag="slot%d" % slot, align_bytes=64)

        def mx_tiles(name, width, tag):
            codes = keep.tile([P, width], U32, name=name + "_codes", tag=tag, align_bytes=64)
            scales = keep.tile([P, width], U8, name=name + "_scales", align_bytes=64)
            return codes, scales

        def quantize(grouped, name, tag=""):
            codes, scales = mx_tiles(name, grouped.shape[1] // PACK, tag or name + "_codes")
            nc.vector.quantize_mx(out=codes[:].bitcast(FP8X4), scales=scales[:], in_=grouped)
            return codes, scales

        offs_sb = keep.tile([P, S // 16], U16, name="offs_sb")
        nc.sync.dma_start(offs_sb[:], offs)

        tab_sc = keep.tile([P, T], U8, name="tab_sc", align_bytes=64)
        nc.vector.memset(tab_sc[:].bitcast(I32), 0)
        sc_rows = tab_scales.rearrange("a (g e) t -> e g a t", e=2)

        warm = lent.tile([P, 4 * PACK], F32, name="warm", offset=24 * J)
        nc.vector.memset(warm[:], 0.0)
        nc.scalar.activation(warm[:], warm[:], ACT.Sin)

        def load_table(words, a, cols):
            nc.sync.dma_start(words[:, cols].bitcast(I32), tab_words[a, :, cols, :].rearrange("p t i -> p (t i)").bitcast(I32))

        def load_rows(slot, w, a, cols, name):
            raw = staged(slot, [P, PACK, BANK], F32, name)
            nc.sync.dma_start(raw[:], w[a * PASS : (a + 1) * PASS, cols].rearrange("(p i) c -> p i c", i=PACK))
            return raw

        def load_w1(a, b):
            return load_rows(a + 1 - b, w1, a, slice(b * PASS, (b + 1) * PASS), "w1_raw%d%d" % (a, b))

        tab0 = staged(0, [P, T], U32, "tab0")
        load_table(tab0, 0, slice(0, T // 2))
        for e in range(2):
            nc.sync.dma_start(tab_sc[e:P:PLANE_STEP, :].bitcast(I32), sc_rows[e].bitcast(I32))
        load_table(tab0, 0, slice(T // 2, T))
        w1_raw = {(a, 0): load_w1(a, 0) for a in range(2)}
        tab1 = staged(3, [P, T], U32, "tab1")
        load_table(tab1, 1, slice(0, T))

        pos1_sb = keep.tile([P, J // 16], U16, name="pos1_sb")
        nc.sync.dma_start(pos1_sb[:], pos1)
        pos2_sb = keep.tile([P, J // 16], U16, name="pos2_sb")
        nc.sync.dma_start(pos2_sb[:], pos2)

        gain_sb = lent.tile([P, 2, PACK], F32, name="gain_sb", offset=24 * J)
        nc.gpsimd.dma_start(gain_sb[:], gain.rearrange("(b p t) -> p b t", b=2, t=PACK))
        rate_sb = lent.tile([P, 2, PACK], F32, name="rate_sb", offset=24 * J + 32)
        nc.gpsimd.dma_start(rate_sb[:], rate.rearrange("(b p t) -> p b t", b=2, t=PACK))
        w3_sc = keep.tile([P, 2, N], U8, name="w3_sc", align_bytes=64)
        nc.vector.memset(w3_sc[:].bitcast(I32), 0)
        w3_rows = w3_scales.rearrange("b (d r) n -> r d b n", r=4)
        for r in range(4):
            nc.gpsimd.dma_start(w3_sc[r:P:32, :, :].bitcast(I32), w3_rows[r].bitcast(I32))

        picked_sc = keep.tile([P, S], U8, name="picked_sc", align_bytes=64)
        nc.vector.tensor_copy(picked_sc[:], tab_sc[:].indirect(offs_sb[:]))
        v_sc = keep.tile([P, S], U8, name="v_sc", align_bytes=64)
        nc.vector.tensor_copy(v_sc[:].bitcast(I32), picked_sc[:].bitcast(I32))
        for a in range(2):
            for e in range(2):
                row = PLANE_STEP * a + e
                nc.scalar.dma_start(v_sc[row + 2 : P : 32, :].bitcast(I32), picked_sc[row + 16 : P : 32, :].bitcast(I32))

        def gather_table(words, name, step):
            picked = keep.tile([P, S], U32, name=name, tag=name, align_bytes=64)
            for m in range(0, S, step):
                nc.vector.tensor_copy(picked[:, m : m + step], words[:].indirect(offs_sb[:, m // 16 : (m + step) // 16]))
            return picked

        def group_w1(a, b, vector_share):
            if (a, b) == (1, 1):
                grouped = lent.tile([P, PACK, P, PACK], BF16, name="w1_bf11", align_bytes=64, offset=4 * J)
            else:
                tag = "v_codes1" if a == 1 else "w1_bf0"
                grouped = keep.tile([P, PACK, P, PACK], BF16, name="w1_bf%d%d" % (a, b), tag=tag, align_bytes=64)
            dst = grouped[:].rearrange("p t m i -> p m i t")
            src = w1_raw[(a, b)][:].rearrange("p i (m t) -> p m i t", t=PACK)
            if vector_share < P:
                nc.scalar.copy(dst[:, vector_share:P], src[:, vector_share:P])
            if vector_share > 0:
                nc.vector.tensor_copy(dst[:, 0:vector_share], src[:, 0:vector_share])
            return grouped[:].rearrange("p t m i -> p (t m i)")

        def interleave(planes, grouped):
            nc.scalar.copy(grouped.rearrange("p (c q) i -> p c i q", q=4), planes[:].rearrange("p i (c q) -> p c i q", q=4))

        def interleave_on_gpsimd(planes, grouped):
            for c in range(0, BANK, GPSIMD_COLUMNS):
                cols = slice(c, c + GPSIMD_COLUMNS)
                nc.gpsimd.tensor_scalar(
                    grouped[:, cols, :], planes[:, :, cols].rearrange("p i c -> p c i"), 1.0, 0.0, ALU.mult, ALU.add
                )

        v_codes = [gather_table(tab0, "v_codes0", S)]
        w1_mx = {(a, 0): quantize(group_w1(a, 0, W1_VECTOR_SHARE[a]), "w1_%d0" % a) for a in range(2)}
        v_codes.append(gather_table(tab1, "v_codes1", BANK))
        for a in range(2):
            w1_raw[(a, 1)] = load_w1(a, 1)
        w2_raw = [load_rows(2 + b, w2, b, slice(0, N), "w2_raw%d" % b) for b in range(2)]

        def first_product(acc, a, b, t, half):
            codes, scales = w1_mx[(a, b)]
            rows = slice(t * P, (t + 1) * P)
            cols = slice(half * BANK, (half + 1) * BANK)
            nc.tensor.matmul_mx(
                out=acc[:],
                lhsT=codes[:, rows].bitcast(FP8X4),
                lhsT_scale=scales[:, rows],
                rhs=v_codes[a][:, cols].bitcast(FP8X4),
                rhs_scale=v_sc[PLANE_STEP * a : P, cols],
                start=(a == 0),
                stop=(a == 1),
            )

        def evacuate(acc, h, b, t, half, on_vector):
            dst = h[:, half * BANK : (half + 1) * BANK]
            if on_vector:
                nc.vector.tensor_scalar(dst, acc[:], gain_sb[:, b, t : t + 1], None, ALU.mult)
            else:
                nc.scalar.activation(dst, acc[:], ACT.Copy, scale=gain_sb[:, b, t : t + 1])

        h = {(b, t): keep.tile([P, S], F32, name="h%d%d" % (b, t), tag="h%d%d" % (b, t), align_bytes=64) for b in range(2) for t in range(PACK) if (b, t) != (1, 2)}
        cos = [keep.tile([P, PACK, J], F32, name="cos%d" % b) for b in range(2)]
        x1 = {}
        x2 = [keep.tile([P, PACK, J], F32, name="x2_%d" % b) for b in range(2)]

        def gather_h(b, t):
            if (b, t) == (0, 3):
                x1[(b, t)] = lent.tile([P, J], F32, name="x1_03", align_bytes=64, offset=4 * J)
            else:
                tag = "w1_bf0" if (b, t) == (0, 2) else "x1_%d%d" % (b, t)
                x1[(b, t)] = keep.tile([P, J], F32, name="x1_%d%d" % (b, t), tag=tag, align_bytes=64)
            nc.vector.tensor_copy(x1[(b, t)][:], h[(b, t)][:].indirect(pos1_sb[:]))
            nc.vector.tensor_copy(x2[b][:, t, :], h[(b, t)][:].indirect(pos2_sb[:]))

        def cosine(b, t):
            angle = x1[(b, t)][:]
            nc.scalar.activation(angle, angle, ACT.Abs, scale=rate_sb[:, b, t : t + 1])
            nc.scalar.activation(cos[b][:, t, :], angle, ACT.Sin, scale=-1.0, bias=math.pi / 2)

        def project(b, grouped):
            step = J
            for c in range(0, J, step):
                cols = slice(c, c + step)
                (nc.gpsimd if b == 0 else nc.vector).tensor_tensor(
                    grouped[:, cols, :].rearrange("p (c q) t -> p c t q", q=2),
                    cos[b][:, :, cols].rearrange("p t (c q) -> p c t q", q=2),
                    x2[b][:, :, cols].rearrange("p t (c q) -> p c t q", q=2),
                    ALU.mult,
                )

        def h_slice(b, t, passes):
            for half in range(2):
                if (b, t, half) not in acc:
                    acc[(b, t, half)] = bank(2 * (t % 2) + half, "h_acc%d%d%d" % (b, t, half))
                for a in passes:
                    first_product(acc[(b, t, half)], a, b, t, half)

        acc = {}
        for t in range(2):
            h_slice(0, t, [0])
        for t in range(PACK):
            h_slice(0, t, [1] if t < 2 else [0, 1])
            for half in range(2):
                evacuate(acc[(0, t, half)], h[(0, t)], 0, t, half, t == 0 and half == 1)
            gather_h(0, t)
            if t in (1, 2):
                w1_mx[(t - 1, 1)] = quantize(group_w1(t - 1, 1, 0), "w1_%d1" % (t - 1))

        load_sb = staged(0, [P, N // P, J], F32, "load_sb")
        nc.sync.dma_start(load_sb[:], load.rearrange("(n p) j -> p n j", p=P))
        w3_sb = staged(1, [P, 2, 2 * N], U8, "w3_sb")
        nc.sync.dma_start(w3_sb[:].bitcast(I32), w3_words.rearrange("b p c -> p b c").bitcast(I32))

        w2_bf = lent.tile([P, 2, N, PACK], BF16, name="w2_bf", align_bytes=64, offset=8 * J)
        for b in range(2):
            interleave_on_gpsimd(w2_raw[b], w2_bf[:, b])

        h[(1, 2)] = lent.tile([P, S], F32, name="h12", align_bytes=64, offset=0)
        cosine(0, 0)
        cosine(0, 1)
        for t in range(PACK):
            h_slice(1, t, [0, 1])
            for half in range(2):
                evacuate(acc[(1, t, half)], h[(1, t)], 1, t, half, False)
            if t < 2:
                cosine(0, t + 2)
            gather_h(1, t)

        w2_codes, w2_scales = quantize(w2_bf[:].rearrange("p b n i -> p (b n i)"), "w2", "h13")
        turned = [bank(N // P + n, "turned%d" % n) for n in range(N // P)]
        direct = [bank(n, "direct%d" % n) for n in range(N // P)]

        def second_products(b, z_codes, z_scales, x2_codes, x2_scales):
            def turn(n):
                cols = slice(b * N + n * P, b * N + (n + 1) * P)
                nc.tensor.matmul_mx(
                    out=turned[n][:],
                    lhsT=w2_codes[:, cols].bitcast(FP8X4),
                    lhsT_scale=w2_scales[:, cols],
                    rhs=z_codes.bitcast(FP8X4),
                    rhs_scale=z_scales,
                    start=(b == 0),
                    stop=(b == 1),
                )

            def read_direct(n):
                nc.tensor.matmul_mx(
                    out=direct[n][:],
                    lhsT=w3_sb[:, b, 2 * n * P : 2 * (n + 1) * P].bitcast(FP4X4),
                    lhsT_scale=w3_sc[:, b, n * P : (n + 1) * P],
                    rhs=x2_codes.bitcast(FP8X4),
                    rhs_scale=x2_scales,
                    start=(b == 0),
                    stop=(b == 1),
                )

            for n in range(N // P):
                turn(n)
                read_direct(n)

        pair_bf = keep.tile([P, 2, J, PACK], BF16, name="pair_bf", align_bytes=64)
        interleave(x2[0], pair_bf[:, 0])
        project(0, pair_bf[:, 1])
        codes, scales = quantize(pair_bf[:].rearrange("p s j t -> p (s j t)"), "pair0")
        second_products(0, codes[:, J : 2 * J], scales[:, J : 2 * J], codes[:, 0:J], scales[:, 0:J])

        for t in range(PACK):
            cosine(1, t)
        x2_bf = keep.tile([P, J, PACK], BF16, name="x2_bf1", align_bytes=64)
        interleave(x2[1], x2_bf[:])
        z_bf = keep.tile([P, J, PACK], BF16, name="z_bf1", tag="z_bf1", align_bytes=64)
        project(1, z_bf)
        z_codes, z_scales = quantize(z_bf[:].rearrange("p j t -> p (j t)"), "z1")
        x2_codes, x2_scales = quantize(x2_bf[:].rearrange("p j t -> p (j t)"), "x2_1", "z_bf1")
        second_products(1, z_codes[:], z_scales[:], x2_codes[:], x2_scales[:])

        weighted = [keep.tile([P, J], F32, name="weighted%d" % n) for n in range(N // P)]
        result = [keep.tile([P, J], F32, name="result%d" % n) for n in range(N // P)]
        for n in range(N // P + 1):
            if n < N // P:
                nc.vector.tensor_tensor(weighted[n][:], turned[n][:], load_sb[:, n, :], ALU.mult)
            if n > 0:
                nc.vector.tensor_tensor(result[n - 1][:], direct[n - 1][:], weighted[n - 1][:], ALU.add)
                nc.sync.dma_start(out[(n - 1) * P : n * P, :], result[n - 1][:])
